import numpy as np, ml_dtypes
CORES = [4,12,20,28,44,60,76,84,92,108,116,124]
N = 12
import mx_ref
NC = 256
CNT = [[0,8,0,0,24,24,104,32,16,0,48,0],[8,112,0,8,0,8,0,32,24,24,16,24],[24,16,16,8,0,24,16,0,96,48,0,8],[8,0,112,8,8,8,0,8,24,24,32,24],[16,32,16,24,40,96,0,16,0,0,8,8],[8,0,24,0,0,32,40,0,0,136,0,16],[0,0,24,48,96,24,40,0,0,8,8,8],[32,40,0,104,8,8,24,16,0,0,8,16],[0,0,32,16,40,24,16,120,0,0,8,0],[8,32,24,8,0,0,16,0,56,8,96,8],[32,8,0,32,32,8,0,0,8,8,32,96],[120,8,8,0,8,0,0,32,32,0,0,48]]
OFF = [[sum(c[:e]) for e in range(N + 1)] for c in CNT]
BF = ml_dtypes.bfloat16
def setup_inputs(rng):
    def f(*shape):
        return mx_ref.flush((rng.standard_normal(shape, dtype=np.float32) * np.exp2(rng.integers(-2, 3, shape[:-1] + (1,)))).astype(BF))
    return {"w": f(N, 128, 512), "x": f(N, 128, 4 * NC)}
def setup_inputs_blocks(rng):
    d = setup_inputs(rng)
    for k in ("w", "x"): d[k] = mx_ref.spread(d[k], rng, 4)
    return d
def setup_inputs_wide(rng):
    d = setup_inputs(rng)
    for k in ("w", "x"): d[k] = mx_ref.flush((d[k].astype(np.float32) * np.exp2(rng.integers(-8, 9, (N, 1, 1))).astype(np.float32)).astype(BF))
    return d
def setup_inputs_zeros(rng):
    d = setup_inputs(rng); v = d["x"].reshape(N, 128, -1, 4).copy()
    v[np.broadcast_to((rng.random((N, 1, v.shape[2], 1)) < 0.33), v.shape)] = 0
    d["x"] = v.reshape(d["x"].shape)
    return d
def reference(w, x):
    y = np.zeros((N, 128, NC), np.float32)
    for e in range(N):
        t = np.concatenate([x[j][:, 4 * OFF[j][e]:4 * OFF[j][e + 1]] for j in range(N)], axis=1)
        p = mx_ref.matmul(mx_ref.quantize(w[e]), mx_ref.quantize(t)); c = 0
        for j in range(N):
            a, b = OFF[j][e], OFF[j][e + 1]
            y[j][:, a:b] = p[:, c:c + b - a]; c += b - a
    return {"y": y}

from concourse.bass import DstId, RemoteDMATransfer
from concourse.mybir import dt, ActivationFunctionType

NR = 12
WC = 128
XC = 256
BANKS = 8
BANK = 512
DIRECT = 3
PER_HELPER = 2
ON_ENGINES = 16
OFF_ENGINES = 8

SCRATCH = {
    "wb": ("sbuf", [128, 4 * WC], "bfloat16"),
    "xb": ("sbuf", [128, 4 * XC], "bfloat16"),
    "wq": ("sbuf", [128, NR * WC], "float8_e4m3fn_x4"),
    "ws": ("sbuf", [128, NR * WC], "uint8"),
    "xq": ("sbuf", [128, XC], "float8_e4m3fn_x4"),
    "xs": ("sbuf", [128, XC], "uint8"),
    "yb": ("sbuf", [128, XC], "float32"),
    "ps": ("psum", [128, BANKS * BANK], "float32"),
}
SEMAPHORES = (["wl", "xl", "wqd", "xqd", "hs", "hc", "sent", "st", "cpall"]
              + ["a%d" % e for e in range(NR)]
              + ["m%d" % k for k in range(NR)]
              + ["c%d" % k for k in range(NR)])

_CACHE = {}


def _pick(mask, n):
    out, b = 0, 1
    while n and b <= mask:
        if mask & b:
            out |= b
            n -= 1
        b <<= 1
    return out


def _bits(mask):
    n = 0
    while mask:
        n += mask & 1
        mask >>= 1
    return n


def _links(topo, src, dst):
    a, b, d = topo.chip(src), topo.chip(dst), topo.die(src)
    out = []
    if a == b:
        return out
    if not topo.same_plane(a, b):
        out.append(("mate", a, d))
        a = [c for c in range(topo.CHIPS) if topo.mates(a, c)][0]
    if a != b:
        out.append(("out", a, d))
        out.append(("in", b, d))
    return out


def _plan(T, topo):
    if "plan" in _CACHE:
        return _CACHE["plan"]
    cores, cnt = list(T.cores), T.tables["CNT"]
    n = len(cores)
    every = range(topo.CHIPS * topo.CORES_PER_CHIP)
    senders, assign, wants = {}, {}, {}
    for e in range(n):
        r = cores[e]
        want = [j for j in range(n) if j != e and cnt[j][e] > 0]
        near = [j for j in want if topo.may_write(r, cores[j])]
        first = near[:DIRECT]
        rest = [j for j in want if j not in first]
        able = [c for c in every if topo.chip(c) == topo.chip(r) and c != r and c not in cores
                and all(topo.may_write(c, cores[j]) for j in want)]
        far_die = [c for c in able if topo.die(c) != topo.die(r)]
        own_die = [c for c in able if topo.die(c) == topo.die(r)]
        turn = []
        while far_die or own_die:
            if far_die:
                turn.append(far_die.pop(0))
            if own_die:
                turn.append(own_die.pop(0))
        hs = turn[:min(len(turn), -(-len(rest) // PER_HELPER))]
        for j in first:
            assign[(e, j)] = r
        for i, j in enumerate(rest):
            assign[(e, j)] = hs[i % len(hs)]
        senders[e], wants[e] = hs, want

    def weight():
        load = {}
        for (e, j), s in assign.items():
            for l in _links(topo, s, cores[j]):
                load[l] = load.get(l, 0) + 1
        return sum(v ** 3 for v in load.values())

    best, better = weight(), True
    while better:
        better = False
        for e in range(n):
            for x in range(len(wants[e])):
                for y in range(x + 1, len(wants[e])):
                    j1, j2 = wants[e][x], wants[e][y]
                    s1, s2 = assign[(e, j1)], assign[(e, j2)]
                    if s1 == s2 or not (topo.may_write(s1, cores[j2]) and topo.may_write(s2, cores[j1])):
                        continue
                    assign[(e, j1)], assign[(e, j2)] = s2, s1
                    w = weight()
                    if w < best:
                        best, better = w, True
                    else:
                        assign[(e, j1)], assign[(e, j2)] = s1, s2
    direct, helpers, role, when = {}, {}, {}, {}
    for e in range(n):
        direct[e] = [j for j in wants[e] if assign[(e, j)] == cores[e]]
        helpers[e] = [(h, [j for j in wants[e] if assign[(e, j)] == h]) for h in senders[e]]
        for h, js in helpers[e]:
            role[h] = (e, js)
            for i, j in enumerate(js):
                when[(e, j)] = (2, i)
        for i, j in enumerate(direct[e]):
            when[(e, j)] = (1, i)
    order = {}
    for j in range(n):
        es = [e for e in range(n) if e != j and cnt[j][e] > 0]
        es.sort(key=lambda e: when[(e, j)] + (e,))
        order[j] = ([j] if cnt[j][j] > 0 else []) + es
    _CACHE["plan"] = (direct, helpers, role, order)
    return _CACHE["plan"]


def _send(g, T, topo, core, dests, e, codes, sem, engines):
    mask = topo.mask(core, dests[0])
    for d in dests:
        mask &= topo.mask(core, d)
    mask = _pick(mask, engines)

    def view():
        if codes:
            return T.wq[:, e * WC:(e + 1) * WC].bitcast(dt.uint8)
        return T.ws[:, e * WC:(e + 1) * WC]
    ids = [DstId(rid=topo.addr(d)[0], pnc=topo.addr(d)[1]) for d in dests]
    g.remote_dma_fused([RemoteDMATransfer(dst_ids=ids, dma_engine_mask=mask, remote_sem=sem,
                                          srcs=[view()], dsts=[view() for d in dests])], local_sem=T.sem.sent)
    return _bits(mask)


def rank_program(g, core, T, topo):
    direct, helpers, role, order = _plan(T, topo)
    cores = list(T.cores)
    rank = T.rank_of(core)

    if rank is None:
        if core not in role:
            return
        e, js = role[core]
        src = cores[e]
        n_in = _bits(_pick(topo.mask(src, core), ON_ENGINES))
        dests = [cores[j] for j in js]
        g.wait_ge(T.sem.hs, n_in)
        sent = _send(g, T, topo, core, dests, e, False, T.sem["a%d" % e], OFF_ENGINES)
        g.wait_ge(T.sem.hc, n_in)
        sent += _send(g, T, topo, core, dests, e, True, T.sem["a%d" % e], OFF_ENGINES)
        g.wait_ge(T.sem.sent, sent)
        return

    cnt = T.tables["CNT"][rank]
    off = [sum(cnt[:e]) for e in range(NR + 1)]
    mine = slice(rank * WC, (rank + 1) * WC)

    g.sync.dma_start(T.wb[:], T.w[:]).then_inc(T.sem.wl, 16)
    g.sync.dma_start(T.xb[:], T.x[:]).then_inc(T.sem.xl, 16)
    g.vector.wait_ge(T.sem.wl, 16)
    g.vector.quantize_mx(T.wq[:, mine], T.ws[:, mine], T.wb[:]).then_inc(T.sem.wqd, 1)
    g.vector.wait_ge(T.sem.xl, 16)
    g.vector.quantize_mx(T.xq[:], T.xs[:], T.xb[:]).then_inc(T.sem.xqd, 1)

    g.wait_ge(T.sem.wqd, 1)
    sent = 0
    hs = [h for h, js in helpers[rank]]
    if hs:
        sent += _send(g, T, topo, core, hs, rank, False, T.sem.hs, ON_ENGINES)
        sent += _send(g, T, topo, core, hs, rank, True, T.sem.hc, ON_ENGINES)
    ds = [cores[j] for j in direct[rank]]
    if ds:
        sent += _send(g, T, topo, core, ds, rank, False, T.sem["a%d" % rank], OFF_ENGINES)
        sent += _send(g, T, topo, core, ds, rank, True, T.sem["a%d" % rank], OFF_ENGINES)

    todo = order[rank]
    g.tensor.wait_ge(T.sem.xqd, 1)
    last = 0
    for k, e in enumerate(todo):
        a, b = off[e], off[e + 1]
        width = max(128, b - a)
        a0 = min(a, XC - width)
        bank = (k % BANKS) * BANK
        if e == rank:
            g.tensor.wait_ge(T.sem.wqd, 1)
        else:
            g.tensor.wait_ge(T.sem["a%d" % e], 2 * OFF_ENGINES)
        if k >= BANKS:
            g.tensor.wait_ge(T.sem["c%d" % (k - BANKS)], 1)
        g.tensor.matmul_mx(T.ps[:, bank:bank + width], T.wq[:, e * WC:(e + 1) * WC], T.ws[:, e * WC:(e + 1) * WC],
                           T.xq[:, a0:a0 + width], T.xs[:, a0:a0 + width], True, True).then_inc(T.sem["m%d" % k], 1)
        src = T.ps[:, bank + a - a0:bank + b - a0]
        if k + BANKS < len(todo):
            done, n_done = T.sem["c%d" % k], 0
        else:
            done, n_done = T.sem.cpall, 1
        last += n_done
        if k % 2 == 0:
            g.vector.wait_ge(T.sem["m%d" % k], 1)
            g.vector.tensor_copy(T.yb[:, a:b], src).then_inc(done, 1)
        else:
            g.scalar.wait_ge(T.sem["m%d" % k], 1)
            g.scalar.activation(T.yb[:, a:b], src, ActivationFunctionType.Copy).then_inc(done, 1)

    for k in range(len(todo) - BANKS):
        g.sync.wait_ge(T.sem["c%d" % k], 1)
    g.sync.wait_ge(T.sem.cpall, last)
    g.sync.dma_start(T.y[:], T.yb[:]).then_inc(T.sem.st, 16)
    g.sync.wait_ge(T.sem.st, 16)
    if sent:
        g.wait_ge(T.sem.sent, sent)
